import numpy as np, ml_dtypes
CORES = [9,17,57,81,121,137,145,185,209,249]
N = 10
WB, F = 3, 64
def setup_inputs(rng):
    return {"a": rng.standard_normal((N, 128, 128), dtype=np.float32).astype(ml_dtypes.bfloat16), "w": rng.standard_normal((N, 128, F), dtype=np.float32).astype(ml_dtypes.bfloat16)}
def setup_inputs_big(rng):
    d = setup_inputs(rng)
    for k in ("a", "w"): d[k] = (d[k].astype(np.float32) * 1024.0).astype(d[k].dtype)
    return d
def setup_inputs_small(rng):
    d = setup_inputs(rng)
    for k in ("a", "w"): d[k] = (d[k].astype(np.float32) * (1 / 1024.0)).astype(d[k].dtype)
    return d
def setup_inputs_apart(rng):
    d = setup_inputs(rng)
    f = (10.0 ** rng.permutation(np.linspace(-1.5, 1.5, N))).astype(np.float32).reshape(N, 1, 1)
    for k in ("a", "w"): d[k] = (d[k].astype(np.float32) * f).astype(d[k].dtype)
    return d
def reference(a, w):
    A, W = a.astype(np.float64), w.astype(np.float64)
    p = [A[j].T @ W[j] for j in range(N)]
    y = np.stack([sum(p[(r - i) % N] for i in range(WB + 1)) for r in range(N)])
    return {"y": y.astype(ml_dtypes.bfloat16 if a.dtype != np.float64 else np.float64)}

@@ -1,0 +1,126 @@
+from concourse.bass import DstId, RemoteDMATransfer
+from concourse.mybir import AluOpType
+
+WB, F = 3, 64
+
+SCRATCH = {
+    "a_sb": ("sbuf", [128, 128], "bfloat16"),
+    "w_sb": ("sbuf", [128, F], "bfloat16"),
+    "p_ps": ("psum", [128, F], "float32"),
+    "acc1": ("psum", [128, F], "float32"),
+    "acc2": ("psum", [128, F], "float32"),
+    "p_sb": ("sbuf", [128, F], "bfloat16"),
+    "fwd": ("sbuf", [128, F], "bfloat16"),
+    "land1": ("sbuf", [128, F], "bfloat16"),
+    "land2": ("sbuf", [128, F], "bfloat16"),
+    "land3": ("sbuf", [128, F], "bfloat16"),
+    "y_sb": ("sbuf", [128, F], "bfloat16"),
+}
+SEMAPHORES = ["ld", "mm", "cp", "vs", "fin", "st", "sent", "arr", "s1", "s2", "s3"]
+
+
+def _engines(mask):
+    return [e for e in range(mask.bit_length()) if (mask >> e) & 1]
+
+
+def _split(engines, parts):
+    per = 1
+    while per * 2 * parts <= len(engines):
+        per *= 2
+    return [sum(1 << e for e in engines[i * per:(i + 1) * per]) for i in range(parts)], per
+
+
+def _plan(T, topo):
+    cores = list(T.cores)
+    n = len(cores)
+    world = range((max(topo.host(c) for c in cores) + 1) * topo.CORES_PER_HOST)
+    plan = []
+    for j, src in enumerate(cores):
+        readers = [(d, cores[(j + d) % n]) for d in range(1, WB + 1)]
+        near = [(d, r) for d, r in readers if topo.may_write(src, r)]
+        far = [(d, r) for d, r in readers if not topo.may_write(src, r)]
+        idle = [h for h in world
+                if topo.host(h) == topo.host(src) and topo.chip(h) == topo.chip(src) and topo.die(h) == topo.die(src)
+                and h not in cores and all(topo.may_write(h, r) for _, r in far)]
+        leave = 0
+        for _, r in near:
+            leave |= topo.mask(src, r)
+        direct, hand = [], []
+        if near:
+            masks, per = _split(_engines(leave), len(near))
+            direct = [(d, r, masks[i], per) for i, (d, r) in enumerate(near)]
+        if far:
+            inside = [e for e in _engines(topo.mask(src, idle[0])) if not (leave >> e) & 1]
+            masks, per = _split(inside, len(far))
+            for i, (d, r) in enumerate(far):
+                fmask, fper = _split(_engines(topo.mask(idle[i], r)), 1)
+                hand.append((d, r, idle[i], masks[i], per, fmask[0], fper))
+        plan.append((direct, hand))
+    return plan
+
+
+def _transfer(topo, me, to, mask, sem, src, dst):
+    rid, pid = topo.addr(to, me)
+    return RemoteDMATransfer(dst_ids=[DstId(rid=rid, pnc=pid)], dma_engine_mask=mask, remote_sem=sem, src=src, dst=dst)
+
+
+def rank_program(g, core, T, topo):
+    plan = _plan(T, topo)
+    rank = T.rank_of(core)
+
+    if rank is None:
+        for direct, hand in plan:
+            for d, reader, helper, _, per, fmask, fper in hand:
+                if helper == core:
+                    g.wait_ge(T.sem.arr, per)
+                    rid, pid = topo.addr(reader, core)
+                    g.remote_dma(out_ap=T["land%d" % d][:], in_ap=T.fwd[:], remote_sem=T.sem["s%d" % d],
+                                 local_sem=T.sem.sent, pid=pid, routing_id=rid, dma_engine_mask=fmask)
+                    g.wait_ge(T.sem.sent, fper)
+        return
+
+    n = len(T.cores)
+    direct, hand = plan[rank]
+
+    g.sync.dma_start(T.a_sb[:], T.a[:]).then_inc(T.sem.ld, 16)
+    g.scalar.dma_start(T.w_sb[:], T.w[:]).then_inc(T.sem.ld, 16)
+    g.tensor.wait_ge(T.sem.ld, 32)
+    g.tensor.matmul(T.p_ps[:], T.a_sb[:], T.w_sb[:], start=True, stop=True).then_inc(T.sem.mm, 1)
+    g.vector.wait_ge(T.sem.mm, 1)
+    g.vector.tensor_copy(T.p_sb[:], T.p_ps[:]).then_inc(T.sem.cp, 1)
+
+    g.wait_ge(T.sem.cp, 1)
+    left = 0
+    if hand:
+        g.remote_dma_fused([_transfer(topo, core, helper, mask, T.sem.arr, T.p_sb[:], T.fwd[:])
+                            for d, reader, helper, mask, per, _, _ in hand], local_sem=T.sem.sent)
+        left += sum(h[4] for h in hand)
+    if direct:
+        g.remote_dma_fused([_transfer(topo, core, reader, mask, T.sem["s%d" % d], T.p_sb[:], T["land%d" % d][:])
+                            for d, reader, mask, per in direct], local_sem=T.sem.sent)
+        left += sum(x[3] for x in direct)
+
+    due = []
+    for d in range(1, WB + 1):
+        sdirect, shand = plan[(rank - d) % n]
+        for x in sdirect:
+            if x[0] == d:
+                due.append((0, 0, d, x[3]))
+        for h in shand:
+            if h[0] == d:
+                due.append((1, len(shand), d, h[6]))
+    due.sort()
+    chain = [T.p_ps, T.acc1, T.acc2]
+    for i, (_, _, d, count) in enumerate(due):
+        last = i == len(due) - 1
+        g.vector.wait_ge(T.sem["s%d" % d], count)
+        if i:
+            g.vector.wait_ge(T.sem.vs, i)
+        out = T.y_sb if last else chain[i + 1]
+        g.vector.tensor_tensor(out[:], chain[i][:], T["land%d" % d][:], AluOpType.add).then_inc(
+            T.sem.fin if last else T.sem.vs, 1)
+
+    g.sync.wait_ge(T.sem.fin, 1)
+    g.sync.dma_start(T.y[:], T.y_sb[:]).then_inc(T.sem.st, 16)
+    g.sync.wait_ge(T.sem.st, 16)
+    g.wait_ge(T.sem.sent, left)

@@ -1,14 +1,23 @@
 from concourse.bass import DstId, RemoteDMATransfer
 from concourse.mybir import AluOpType
 
-WB, F = 3, 64
+WB, F, K = 3, 64, 128
+BANK = 512
+WENG = 2
 
 SCRATCH = {
-    "a_sb": ("sbuf", [128, 128], "bfloat16"),
+    "a_sb": ("sbuf", [128, K], "bfloat16"),
     "w_sb": ("sbuf", [128, F], "bfloat16"),
-    "p_ps": ("psum", [128, F], "float32"),
-    "acc1": ("psum", [128, F], "float32"),
-    "acc2": ("psum", [128, F], "float32"),
+    "ra1": ("sbuf", [128, K], "bfloat16"),
+    "ra2": ("sbuf", [128, K], "bfloat16"),
+    "ra3": ("sbuf", [128, K], "bfloat16"),
+    "rw1": ("sbuf", [128, F], "bfloat16"),
+    "rw2": ("sbuf", [128, F], "bfloat16"),
+    "rw3": ("sbuf", [128, F], "bfloat16"),
+    "p_ps": ("psum", [128, BANK], "float32"),
+    "y_ps": ("psum", [128, BANK], "float32"),
+    "acc1": ("psum", [128, BANK], "float32"),
+    "acc2": ("psum", [128, BANK], "float32"),
     "p_sb": ("sbuf", [128, F], "bfloat16"),
     "fwd": ("sbuf", [128, F], "bfloat16"),
     "land1": ("sbuf", [128, F], "bfloat16"),
@@ -16,7 +25,7 @@ SCRATCH = {
     "land3": ("sbuf", [128, F], "bfloat16"),
     "y_sb": ("sbuf", [128, F], "bfloat16"),
 }
-SEMAPHORES = ["ld", "mm", "cp", "vs", "fin", "st", "sent", "arr", "s1", "s2", "s3"]
+SEMAPHORES = ["lda", "ldw", "mm", "cp", "ns", "vs", "fin", "st", "sent", "arr", "n1", "n2", "n3", "s1", "s2", "s3"]
 
 
 def _engines(mask):
@@ -45,17 +54,24 @@ def _plan(T, topo):
         leave = 0
         for _, r in near:
             leave |= topo.mask(src, r)
-        direct, hand = [], []
+        raw, direct, hand = None, [], []
         if near:
-            masks, per = _split(_engines(leave), len(near))
-            direct = [(d, r, masks[i], per) for i, (d, r) in enumerate(near)]
+            out = _engines(leave)
+            wlist = out[::len(out) // WENG]
+            rest = [e for e in out if e not in wlist]
+            amasks, aper = _split(rest, 1)
+            raw = (near[0][0], near[0][1], sum(1 << e for e in wlist), WENG, amasks[0], aper)
+            if len(near) > 1:
+                free = [e for e in rest if not (amasks[0] >> e) & 1]
+                masks, per = _split(free if len(free) >= len(near) - 1 else out, len(near) - 1)
+                direct = [(d, r, masks[i], per) for i, (d, r) in enumerate(near[1:])]
         if far:
             inside = [e for e in _engines(topo.mask(src, idle[0])) if not (leave >> e) & 1]
             masks, per = _split(inside, len(far))
             for i, (d, r) in enumerate(far):
                 fmask, fper = _split(_engines(topo.mask(idle[i], r)), 1)
                 hand.append((d, r, idle[i], masks[i], per, fmask[0], fper))
-        plan.append((direct, hand))
+        plan.append((raw, direct, hand))
     return plan
 
 
@@ -69,7 +85,7 @@ def rank_program(g, core, T, topo):
     rank = T.rank_of(core)
 
     if rank is None:
-        for direct, hand in plan:
+        for raw, direct, hand in plan:
             for d, reader, helper, _, per, fmask, fper in hand:
                 if helper == core:
                     g.wait_ge(T.sem.arr, per)
@@ -80,44 +96,74 @@ def rank_program(g, core, T, topo):
         return
 
     n = len(T.cores)
-    direct, hand = plan[rank]
+    raw, direct, hand = plan[rank]
 
-    g.sync.dma_start(T.a_sb[:], T.a[:]).then_inc(T.sem.ld, 16)
-    g.scalar.dma_start(T.w_sb[:], T.w[:]).then_inc(T.sem.ld, 16)
-    g.tensor.wait_ge(T.sem.ld, 32)
-    g.tensor.matmul(T.p_ps[:], T.a_sb[:], T.w_sb[:], start=True, stop=True).then_inc(T.sem.mm, 1)
-    g.vector.wait_ge(T.sem.mm, 1)
-    g.vector.tensor_copy(T.p_sb[:], T.p_ps[:]).then_inc(T.sem.cp, 1)
+    raws, due = [], []
+    for d in range(1, WB + 1):
+        sraw, sdirect, shand = plan[(rank - d) % n]
+        if sraw is not None and sraw[0] == d:
+            raws.append((d, sraw[3] + sraw[5]))
+        for x in sdirect:
+            if x[0] == d:
+                due.append((0, d, x[3]))
+        for h in shand:
+            if h[0] == d:
+                due.append((len(shand), d, h[6]))
+    due.sort()
 
-    g.wait_ge(T.sem.cp, 1)
+    g.scalar.dma_start(T.w_sb[:], T.w[:]).then_inc(T.sem.ldw, 16)
+    g.sync.dma_start(T.a_sb[:], T.a[:]).then_inc(T.sem.lda, 16)
+
     left = 0
+    if raw is not None:
+        d, reader, wmask, wper, amask, aper = raw
+        g.wait_ge(T.sem.ldw, 16)
+        g.remote_dma_fused([_transfer(topo, core, reader, wmask, T.sem["n%d" % d], T.w_sb[:], T["rw%d" % d][:])],
+                           local_sem=T.sem.sent)
+        left += wper
+
+    g.tensor.wait_ge(T.sem.ldw, 16)
+    g.tensor.wait_ge(T.sem.lda, 16)
+    if hand or direct:
+        g.tensor.matmul(T.p_ps[:, 0:F], T.a_sb[:], T.w_sb[:], start=True, stop=True).then_inc(T.sem.mm, 1)
+    last_mm = g.tensor.matmul(T.y_ps[:, 0:F], T.a_sb[:], T.w_sb[:], start=True, stop=not raws)
+    for i, (d, count) in enumerate(raws):
+        g.tensor.wait_ge(T.sem["n%d" % d], count)
+        last_mm = g.tensor.matmul(T.y_ps[:, 0:F], T["ra%d" % d][:], T["rw%d" % d][:], start=False,
+                                  stop=i == len(raws) - 1)
+    last_mm.then_inc(T.sem.ns, 1)
+
+    if hand or direct:
+        g.vector.wait_ge(T.sem.mm, 1)
+        g.vector.tensor_copy(T.p_sb[:], T.p_ps[:, 0:F]).then_inc(T.sem.cp, 1)
+        g.wait_ge(T.sem.cp, 1)
     if hand:
         g.remote_dma_fused([_transfer(topo, core, helper, mask, T.sem.arr, T.p_sb[:], T.fwd[:])
                             for d, reader, helper, mask, per, _, _ in hand], local_sem=T.sem.sent)
         left += sum(h[4] for h in hand)
+
+    if raw is not None:
+        d, reader, wmask, wper, amask, aper = raw
+        g.wait_ge(T.sem.lda, 16)
+        g.remote_dma_fused([_transfer(topo, core, reader, amask, T.sem["n%d" % d], T.a_sb[:], T["ra%d" % d][:])],
+                           local_sem=T.sem.sent)
+        left += aper
     if direct:
         g.remote_dma_fused([_transfer(topo, core, reader, mask, T.sem["s%d" % d], T.p_sb[:], T["land%d" % d][:])
                             for d, reader, mask, per in direct], local_sem=T.sem.sent)
         left += sum(x[3] for x in direct)
 
-    due = []
-    for d in range(1, WB + 1):
-        sdirect, shand = plan[(rank - d) % n]
-        for x in sdirect:
-            if x[0] == d:
-                due.append((0, 0, d, x[3]))
-        for h in shand:
-            if h[0] == d:
-                due.append((1, len(shand), d, h[6]))
-    due.sort()
-    chain = [T.p_ps, T.acc1, T.acc2]
-    for i, (_, _, d, count) in enumerate(due):
+    g.vector.wait_ge(T.sem.ns, 1)
+    if not due:
+        g.vector.tensor_copy(T.y_sb[:], T.y_ps[:, 0:F]).then_inc(T.sem.fin, 1)
+    chain = [T.y_ps, T.acc1, T.acc2]
+    for i, (_, d, count) in enumerate(due):
         last = i == len(due) - 1
         g.vector.wait_ge(T.sem["s%d" % d], count)
         if i:
             g.vector.wait_ge(T.sem.vs, i)
-        out = T.y_sb if last else chain[i + 1]
-        g.vector.tensor_tensor(out[:], chain[i][:], T["land%d" % d][:], AluOpType.add).then_inc(
+        out = T.y_sb[:] if last else chain[i + 1][:, 0:F]
+        g.vector.tensor_tensor(out, chain[i][:, 0:F], T["land%d" % d][:], AluOpType.add).then_inc(
             T.sem.fin if last else T.sem.vs, 1)
 
     g.sync.wait_ge(T.sem.fin, 1)

from concourse.bass import DstId, RemoteDMATransfer
from concourse.mybir import AluOpType

WB, F, K = 3, 64, 128
BANK = 512
WENG = 2

SCRATCH = {
    "a_sb": ("sbuf", [128, K], "bfloat16"),
    "w_sb": ("sbuf", [128, F], "bfloat16"),
    "ra1": ("sbuf", [128, K], "bfloat16"),
    "ra2": ("sbuf", [128, K], "bfloat16"),
    "ra3": ("sbuf", [128, K], "bfloat16"),
    "rw1": ("sbuf", [128, F], "bfloat16"),
    "rw2": ("sbuf", [128, F], "bfloat16"),
    "rw3": ("sbuf", [128, F], "bfloat16"),
    "p_ps": ("psum", [128, BANK], "float32"),
    "y_ps": ("psum", [128, BANK], "float32"),
    "acc1": ("psum", [128, BANK], "float32"),
    "acc2": ("psum", [128, BANK], "float32"),
    "p_sb": ("sbuf", [128, F], "bfloat16"),
    "fwd": ("sbuf", [128, F], "bfloat16"),
    "land1": ("sbuf", [128, F], "bfloat16"),
    "land2": ("sbuf", [128, F], "bfloat16"),
    "land3": ("sbuf", [128, F], "bfloat16"),
    "y_sb": ("sbuf", [128, F], "bfloat16"),
}
SEMAPHORES = ["lda", "ldw", "mm", "cp", "ns", "vs", "fin", "st", "sent", "arr", "n1", "n2", "n3", "s1", "s2", "s3"]


def _engines(mask):
    return [e for e in range(mask.bit_length()) if (mask >> e) & 1]


def _split(engines, parts):
    per = 1
    while per * 2 * parts <= len(engines):
        per *= 2
    return [sum(1 << e for e in engines[i * per:(i + 1) * per]) for i in range(parts)], per


def _plan(T, topo):
    cores = list(T.cores)
    n = len(cores)
    world = range((max(topo.host(c) for c in cores) + 1) * topo.CORES_PER_HOST)
    plan = []
    for j, src in enumerate(cores):
        readers = [(d, cores[(j + d) % n]) for d in range(1, WB + 1)]
        near = [(d, r) for d, r in readers if topo.may_write(src, r)]
        far = [(d, r) for d, r in readers if not topo.may_write(src, r)]
        idle = [h for h in world
                if topo.host(h) == topo.host(src) and topo.chip(h) == topo.chip(src) and topo.die(h) == topo.die(src)
                and h not in cores and all(topo.may_write(h, r) for _, r in far)]
        leave = 0
        for _, r in near:
            leave |= topo.mask(src, r)
        raw, direct, hand = None, [], []
        if near:
            out = _engines(leave)
            wlist = out[::len(out) // WENG]
            rest = [e for e in out if e not in wlist]
            amasks, aper = _split(rest, 1)
            raw = (near[0][0], near[0][1], sum(1 << e for e in wlist), WENG, amasks[0], aper)
            if len(near) > 1:
                free = [e for e in rest if not (amasks[0] >> e) & 1]
                masks, per = _split(free if len(free) >= len(near) - 1 else out, len(near) - 1)
                direct = [(d, r, masks[i], per) for i, (d, r) in enumerate(near[1:])]
        if far:
            inside = [e for e in _engines(topo.mask(src, idle[0])) if not (leave >> e) & 1]
            masks, per = _split(inside, len(far))
            for i, (d, r) in enumerate(far):
                fmask, fper = _split(_engines(topo.mask(idle[i], r)), 1)
                hand.append((d, r, idle[i], masks[i], per, fmask[0], fper))
        plan.append((raw, direct, hand))
    return plan


def _transfer(topo, me, to, mask, sem, src, dst):
    rid, pid = topo.addr(to, me)
    return RemoteDMATransfer(dst_ids=[DstId(rid=rid, pnc=pid)], dma_engine_mask=mask, remote_sem=sem, src=src, dst=dst)


def rank_program(g, core, T, topo):
    plan = _plan(T, topo)
    rank = T.rank_of(core)

    if rank is None:
        for raw, direct, hand in plan:
            for d, reader, helper, _, per, fmask, fper in hand:
                if helper == core:
                    g.wait_ge(T.sem.arr, per)
                    rid, pid = topo.addr(reader, core)
                    g.remote_dma(out_ap=T["land%d" % d][:], in_ap=T.fwd[:], remote_sem=T.sem["s%d" % d],
                                 local_sem=T.sem.sent, pid=pid, routing_id=rid, dma_engine_mask=fmask)
                    g.wait_ge(T.sem.sent, fper)
        return

    n = len(T.cores)
    raw, direct, hand = plan[rank]

    raws, due = [], []
    for d in range(1, WB + 1):
        sraw, sdirect, shand = plan[(rank - d) % n]
        if sraw is not None and sraw[0] == d:
            raws.append((d, sraw[3] + sraw[5]))
        for x in sdirect:
            if x[0] == d:
                due.append((0, d, x[3]))
        for h in shand:
            if h[0] == d:
                due.append((len(shand), d, h[6]))
    due.sort()

    g.scalar.dma_start(T.w_sb[:], T.w[:]).then_inc(T.sem.ldw, 16)
    g.sync.dma_start(T.a_sb[:], T.a[:]).then_inc(T.sem.lda, 16)

    left = 0
    if raw is not None:
        d, reader, wmask, wper, amask, aper = raw
        g.wait_ge(T.sem.ldw, 16)
        g.remote_dma_fused([_transfer(topo, core, reader, wmask, T.sem["n%d" % d], T.w_sb[:], T["rw%d" % d][:])],
                           local_sem=T.sem.sent)
        left += wper

    g.tensor.wait_ge(T.sem.ldw, 16)
    g.tensor.wait_ge(T.sem.lda, 16)
    if hand or direct:
        g.tensor.matmul(T.p_ps[:, 0:F], T.a_sb[:], T.w_sb[:], start=True, stop=True).then_inc(T.sem.mm, 1)
    last_mm = g.tensor.matmul(T.y_ps[:, 0:F], T.a_sb[:], T.w_sb[:], start=True, stop=not raws)
    for i, (d, count) in enumerate(raws):
        g.tensor.wait_ge(T.sem["n%d" % d], count)
        last_mm = g.tensor.matmul(T.y_ps[:, 0:F], T["ra%d" % d][:], T["rw%d" % d][:], start=False,
                                  stop=i == len(raws) - 1)
    last_mm.then_inc(T.sem.ns, 1)

    if hand or direct:
        g.vector.wait_ge(T.sem.mm, 1)
        g.vector.tensor_copy(T.p_sb[:], T.p_ps[:, 0:F]).then_inc(T.sem.cp, 1)
        g.wait_ge(T.sem.cp, 1)
    if hand:
        g.remote_dma_fused([_transfer(topo, core, helper, mask, T.sem.arr, T.p_sb[:], T.fwd[:])
                            for d, reader, helper, mask, per, _, _ in hand], local_sem=T.sem.sent)
        left += sum(h[4] for h in hand)

    if raw is not None:
        d, reader, wmask, wper, amask, aper = raw
        g.wait_ge(T.sem.lda, 16)
        g.remote_dma_fused([_transfer(topo, core, reader, amask, T.sem["n%d" % d], T.a_sb[:], T["ra%d" % d][:])],
                           local_sem=T.sem.sent)
        left += aper
    if direct:
        g.remote_dma_fused([_transfer(topo, core, reader, mask, T.sem["s%d" % d], T.p_sb[:], T["land%d" % d][:])
                            for d, reader, mask, per in direct], local_sem=T.sem.sent)
        left += sum(x[3] for x in direct)

    g.vector.wait_ge(T.sem.ns, 1)
    if not due:
        g.vector.tensor_copy(T.y_sb[:], T.y_ps[:, 0:F]).then_inc(T.sem.fin, 1)
    chain = [T.y_ps, T.acc1, T.acc2]
    for i, (_, d, count) in enumerate(due):
        last = i == len(due) - 1
        g.vector.wait_ge(T.sem["s%d" % d], count)
        if i:
            g.vector.wait_ge(T.sem.vs, i)
        out = T.y_sb[:] if last else chain[i + 1][:, 0:F]
        g.vector.tensor_tensor(out, chain[i][:, 0:F], T["land%d" % d][:], AluOpType.add).then_inc(
            T.sem.fin if last else T.sem.vs, 1)

    g.sync.wait_ge(T.sem.fin, 1)
    g.sync.dma_start(T.y[:], T.y_sb[:]).then_inc(T.sem.st, 16)
    g.sync.wait_ge(T.sem.st, 16)
    g.wait_ge(T.sem.sent, left)
